import numpy as np
import ml_dtypes


def mxq(x, axis, fmt="e4m3"):
    dtype, down = {"e4m3": (ml_dtypes.float8_e4m3fn, 7), "e5m2": (ml_dtypes.float8_e5m2, 14)}[fmt]
    v = np.moveaxis(np.asarray(x, np.float32).astype(ml_dtypes.bfloat16).astype(np.float64), axis, -1)
    blocks = v.reshape(v.shape[:-1] + (-1, 32))
    amax = np.abs(blocks).max(-1, keepdims=True)
    byte = np.maximum(np.where(amax > 0, np.frexp(amax)[1] - 1 + 127, 0) - down, 1)
    scale = np.exp2(byte - 127.0)
    codes = (blocks / scale).astype(np.float32).astype(dtype).astype(np.float64)
    return np.moveaxis((codes * scale).reshape(v.shape), -1, axis)


WIDE = False


def mx_kscale(k):
    if not WIDE:
        return np.ones(k)
    levels = np.array([10, -10, 5, -5, 0])
    if k % 512:
        return np.exp2(np.random.permutation(np.resize(levels, k // 32))).repeat(32)
    a = np.empty((k // 512, 16))
    for p in range(k // 512):
        a[p, :8] = np.random.permutation(np.resize(levels, 8))
        for g in range(8):
            far = levels[np.abs(levels - a[p, g]) >= 10]
            a[p, g + 8] = far[np.random.randint(len(far))]
    return np.exp2(a.ravel()).repeat(32)


def f64(x):
    return np.asarray(x).astype(np.float64)


def striped(idx):
    return np.tile(idx.reshape(-1, 16).T, (8, 1)).astype(np.uint16)


def unstriped(offs):
    return offs[:16].T.reshape(-1).astype(np.int64)


def relu(v):
    return np.maximum(v, 0.0)


K, T, E, C, H, N = 1536, 512, 4, 128, 1024, 384


def by_expert(wq, xq):
    return np.concatenate([wq[e].T @ xq[:, e * C:(e + 1) * C] for e in range(E)], axis=1)


def setup_inputs():
    n = np.random.standard_normal
    s = mx_kscale(K)[:, None]
    u = mx_kscale(H)
    return {
        "xT": (n((K, T)) * s).astype(np.float32),
        "w1": (n((E, K, H)) / np.sqrt(K) / s[None] * u[None, None, :]).astype(np.float32),
        "w2": (n((E, H, N)) / np.sqrt(H) / u[None, :, None]).astype(np.float32),
        "gate": np.tile(np.random.uniform(0.2, 1.0, E * C), (N, 1)).astype(np.float32),
        "offs": striped(np.random.permutation(T)[:E * C]),
    }


def reference(xT, w1, w2, gate, offs):
    idx = unstriped(offs)
    xq = mxq(f64(xT)[:, idx], 0, "e4m3")
    h = relu(by_expert(mxq(f64(w1), 1, "e4m3"), xq))
    y = by_expert(mxq(f64(w2), 1, "e4m3"), mxq(h, 0, "e4m3"))
    out = np.zeros((N, T))
    out[:, idx] = f64(gate) * y
    return out

@@ -1,0 +1,213 @@
+from contextlib import ExitStack
+
+import concourse.mybir as mybir
+
+K, T, E, C, H, N = 1536, 512, 4, 128, 1024, 384
+FLOPS = 2 * E * C * (K * H + H * N)
+
+F32 = mybir.dt.float32
+BF16 = mybir.dt.bfloat16
+U32 = mybir.dt.uint32
+U16 = mybir.dt.uint16
+U8 = mybir.dt.uint8
+FP8X4 = mybir.dt.float8_e4m3fn_x4
+RELU = mybir.ActivationFunctionType.Relu
+MULT = mybir.AluOpType.mult
+
+P = 128
+PACK = 4
+K_PASS = P * PACK
+K_PASSES = K // K_PASS
+H_PASSES = H // K_PASS
+N_TILES = N // P
+SHARE = 40
+LAST_SHARE = 72
+RAW_COLS = PACK * H
+
+
+def tile_routed_moe_kernel(tc, xT, w1, w2, gate, offs, out):
+    nc = tc.nc
+
+    with ExitStack() as ctx:
+        keep = ctx.enter_context(tc.tile_pool(name="keep", bufs=1))
+        ring = ctx.enter_context(tc.tile_pool(name="ring", bufs=6))
+        mid = ctx.enter_context(tc.tile_pool(name="mid", bufs=3))
+        codes = ctx.enter_context(tc.tile_pool(name="codes", bufs=2))
+        psum = ctx.enter_context(tc.psum_pool(name="psum", bufs=2))
+
+        offsets = keep.tile([P, E * C // 16], U16, name="offsets")
+        gate_sb = keep.tile([P, N_TILES, E * C], F32, name="gate_sb")
+        windows = [keep.tile([P, T], F32, name=f"window{n}") for n in range(N_TILES)]
+        x_words = [keep.tile([P, T], U32, name=f"x_words{s}", align_bytes=64) for s in range(K_PASSES)]
+        x_bytes = [keep.tile([P, T], U8, name=f"x_bytes{s}", align_bytes=64) for s in range(K_PASSES)]
+        g_words = [keep.tile([P, E * C], U32, name=f"g_words{s}", align_bytes=64) for s in range(K_PASSES)]
+        g_bytes = [keep.tile([P, E * C], U8, name=f"g_bytes{s}", align_bytes=64) for s in range(K_PASSES)]
+
+        def load(rows, width):
+            raw = ring.tile([P, RAW_COLS], F32, name="raw")
+            view = raw[:, : PACK * width].rearrange("p (j w) -> p j w", j=PACK)
+            nc.sync.dma_start(view, rows.rearrange("(p j) w -> p j w", j=PACK))
+            return view
+
+        def interleave(copy, grouped, view):
+            copy(
+                grouped.rearrange("p (c i j) -> p c j i", i=PACK, j=PACK),
+                view.rearrange("p j (c i) -> p c j i", i=PACK),
+            )
+
+        def interleave_permuted(copy, grouped, view, m0, m1):
+            copy(
+                grouped.rearrange("p (b t m j) -> p b m j t", t=PACK, m=P, j=PACK)[:, :, m0:m1],
+                view.rearrange("p j (b m t) -> p b m j t", m=P, t=PACK)[:, :, m0:m1],
+            )
+
+        for s in range(K_PASSES):
+            nc.gpsimd.memset(x_bytes[s][:], 0)
+        for s in range(K_PASSES):
+            view = load(xT[K_PASS * s : K_PASS * (s + 1), :], T)
+            if s == 0:
+                nc.sync.dma_start(offsets[:], offs)
+            half = T // 2
+            for i, copy in enumerate((nc.vector.tensor_copy, nc.scalar.copy)):
+                cols = slice(half * i, half * (i + 1))
+                grouped = mid.tile([P, PACK * half], BF16, name=f"x_grouped{i}", align_bytes=64)
+                interleave(copy, grouped[:], view[:, :, cols])
+                nc.vector.quantize_mx(
+                    out=x_words[s][:, cols].bitcast(FP8X4), scales=x_bytes[s][:, cols], in_=grouped[:]
+                )
+        for s in range(K_PASSES):
+            for g0 in range(0, E * C, 256):
+                some = offsets[:, g0 // 16 : (g0 + 256) // 16]
+                nc.vector.tensor_copy(g_words[s][:, g0 : g0 + 256], x_words[s][:].indirect(some))
+                nc.vector.tensor_copy(g_bytes[s][:, g0 : g0 + 256], x_bytes[s][:].indirect(some))
+
+        def first_layer(e):
+            slots = slice(C * e, C * (e + 1))
+            w_words, w_bytes, grouped_tiles = [], [], []
+
+            def quantize(s, c0, c1):
+                nc.vector.quantize_mx(
+                    out=w_words[s][:, c0:c1].bitcast(FP8X4),
+                    scales=w_bytes[s][:, c0:c1],
+                    in_=grouped_tiles[s][:, PACK * c0 : PACK * c1],
+                )
+
+            for s in range(K_PASSES):
+                rows = w1[e, K_PASS * s : K_PASS * (s + 1), :]
+                w_words.append(codes.tile([P, H], U32, name=f"w1_words{s}", align_bytes=64))
+                w_bytes.append(codes.tile([P, H], U8, name=f"w1_bytes{s}", align_bytes=64))
+                grouped = mid.tile([P, PACK * H], BF16, name="w1_grouped", align_bytes=64)
+                grouped_tiles.append(grouped)
+                if e == E - 1 and s == K_PASSES - 1:
+                    quantize(s - 1, 0, H)
+                    for b in range(H_PASSES):
+                        half = load(rows[:, K_PASS * b : K_PASS * (b + 1)], K_PASS)
+                        part = grouped[:, PACK * K_PASS * b : PACK * K_PASS * (b + 1)]
+                        interleave_permuted(nc.vector.tensor_copy, part, half, 0, LAST_SHARE)
+                        interleave_permuted(nc.scalar.copy, part, half, LAST_SHARE, P)
+                        quantize(s, K_PASS * b, K_PASS * (b + 1))
+                else:
+                    view = load(rows, H)
+                    interleave_permuted(nc.vector.tensor_copy, grouped[:], view, 0, SHARE)
+                    interleave_permuted(nc.scalar.copy, grouped[:], view, SHARE, P)
+                    if s > 0:
+                        quantize(s - 1, 0, H)
+                    if s == K_PASSES - 1:
+                        quantize(s, 0, H)
+            hidden = []
+            for b in range(H_PASSES):
+                acc = psum.tile([P, PACK, C], F32, name=f"h_acc{b}")
+                for t in range(PACK):
+                    cols = slice(K_PASS * b + P * t, K_PASS * b + P * (t + 1))
+                    for s in range(K_PASSES):
+                        nc.tensor.matmul_mx(
+                            out=acc[:, t, :],
+                            lhsT=w_words[s][:, cols].bitcast(FP8X4),
+                            lhsT_scale=w_bytes[s][:, cols],
+                            rhs=g_words[s][:, slots].bitcast(FP8X4),
+                            rhs_scale=g_bytes[s][:, slots],
+                            start=(s == 0),
+                            stop=(s == K_PASSES - 1),
+                        )
+                h_grouped = codes.tile([P, C, PACK], BF16, name=f"h_grouped{b}", align_bytes=64)
+                nc.scalar.activation(h_grouped[:], acc[:].rearrange("p t n -> p n t"), RELU)
+                words = codes.tile([P, C], U32, name=f"h_words{b}", align_bytes=64)
+                scales = codes.tile([P, C], U8, name=f"h_bytes{b}", align_bytes=64)
+                nc.vector.quantize_mx(
+                    out=words[:].bitcast(FP8X4), scales=scales[:], in_=h_grouped[:].rearrange("p n t -> p (n t)")
+                )
+                hidden.append((words, scales))
+            return hidden
+
+        def second_matmul(acc, w_words, w_bytes, hidden):
+            for b in range(H_PASSES):
+                nc.tensor.matmul_mx(
+                    out=acc,
+                    lhsT=w_words[b].bitcast(FP8X4),
+                    lhsT_scale=w_bytes[b],
+                    rhs=hidden[b][0][:].bitcast(FP8X4),
+                    rhs_scale=hidden[b][1][:],
+                    start=(b == 0),
+                    stop=(b == H_PASSES - 1),
+                )
+
+        def back(e, n, weighted):
+            nc.vector.tensor_copy(windows[n][:].indirect(offsets[:, C * e // 16 : C * (e + 1) // 16]), weighted)
+
+        def second_layer(e, hidden):
+            slots = slice(C * e, C * (e + 1))
+            raw = ring.tile([P, RAW_COLS], F32, name="raw")
+            view = raw[:, : H_PASSES * PACK * N].rearrange("p (s j n) -> p s j n", s=H_PASSES, j=PACK)
+            nc.sync.dma_start(view, w2[e].rearrange("(s p j) n -> p s j n", s=H_PASSES, j=PACK))
+            width = PACK * N
+            grouped = codes.tile([P, H_PASSES * width], BF16, name="w2_grouped", align_bytes=64)
+            words = codes.tile([P, H_PASSES * N], U32, name="w2_words", align_bytes=64)
+            scales = codes.tile([P, H_PASSES * N], U8, name="w2_bytes", align_bytes=64)
+            for s in range(H_PASSES):
+                interleave(nc.scalar.copy, grouped[:, width * s : width * (s + 1)], view[:, s])
+            for c0, c1 in ((0, 512), (512, 768)):
+                nc.vector.quantize_mx(
+                    out=words[:, c0:c1].bitcast(FP8X4), scales=scales[:, c0:c1], in_=grouped[:, PACK * c0 : PACK * c1]
+                )
+            acc = psum.tile([P, N_TILES, C], F32, name="y_acc")
+            for n in range(N_TILES):
+                cols = [slice(N * b + P * n, N * b + P * (n + 1)) for b in range(H_PASSES)]
+                second_matmul(acc[:, n, :], [words[:, c] for c in cols], [scales[:, c] for c in cols], hidden)
+            weighted = codes.tile([P, N_TILES, C], F32, name="weighted")
+            nc.vector.tensor_tensor(weighted[:], acc[:], gate_sb[:, :, slots], MULT)
+            for n in range(N_TILES):
+                back(e, n, weighted[:, n, :])
+
+        def last_second_layer(e, hidden):
+            slots = slice(C * e, C * (e + 1))
+            acc = psum.tile([P, N_TILES, C], F32, name="y_acc")
+            for n0, n1 in ((0, 2), (2, 3)):
+                width = P * (n1 - n0)
+                w_words, w_bytes = [], []
+                for s, copy in enumerate((nc.scalar.copy, nc.vector.tensor_copy)):
+                    view = load(w2[e, K_PASS * s : K_PASS * (s + 1), P * n0 : P * n1], width)
+                    grouped = codes.tile([P, PACK * width], BF16, name=f"w2_last_grouped{s}", align_bytes=64)
+                    interleave(copy, grouped[:], view)
+                    words = codes.tile([P, width], U32, name=f"w2_last_words{s}", align_bytes=64)
+                    scales = codes.tile([P, width], U8, name=f"w2_last_bytes{s}", align_bytes=64)
+                    nc.vector.quantize_mx(out=words[:].bitcast(FP8X4), scales=scales[:], in_=grouped[:])
+                    w_words.append(words)
+                    w_bytes.append(scales)
+                for n in range(n0, n1):
+                    cols = slice(P * (n - n0), P * (n - n0 + 1))
+                    second_matmul(acc[:, n, :], [w[:, cols] for w in w_words], [w[:, cols] for w in w_bytes], hidden)
+                weighted = codes.tile([P, n1 - n0, C], F32, name="weighted_last")
+                nc.vector.tensor_tensor(weighted[:], acc[:, n0:n1, :], gate_sb[:, n0:n1, slots], MULT)
+                for n in range(n0, n1):
+                    back(e, n, weighted[:, n - n0, :])
+                    nc.sync.dma_start(out[P * n : P * (n + 1), :], windows[n][:])
+
+        h0 = first_layer(0)
+        nc.sync.dma_start(gate_sb[:], gate.rearrange("(n p) j -> p n j", p=P))
+        second_layer(0, h0)
+        h1 = first_layer(1)
+        second_layer(1, h1)
+        h2 = first_layer(2)
+        h3 = first_layer(3)
+        second_layer(2, h2)
+        last_second_layer(3, h3)

@@ -202,12 +202,9 @@ def tile_routed_moe_kernel(tc, xT, w1, w2, gate, offs, out):
                     back(e, n, weighted[:, n - n0, :])
                     nc.sync.dma_start(out[P * n : P * (n + 1), :], windows[n][:])
 
-        h0 = first_layer(0)
+        hidden = first_layer(0)
         nc.sync.dma_start(gate_sb[:], gate.rearrange("(n p) j -> p n j", p=P))
-        second_layer(0, h0)
-        h1 = first_layer(1)
-        second_layer(1, h1)
-        h2 = first_layer(2)
-        h3 = first_layer(3)
-        second_layer(2, h2)
-        last_second_layer(3, h3)
+        for e in range(E - 1):
+            second_layer(e, hidden)
+            hidden = first_layer(e + 1)
+        last_second_layer(E - 1, hidden)

from contextlib import ExitStack

import concourse.mybir as mybir

K, T, E, C, H, N = 1536, 512, 4, 128, 1024, 384
FLOPS = 2 * E * C * (K * H + H * N)

F32 = mybir.dt.float32
BF16 = mybir.dt.bfloat16
U32 = mybir.dt.uint32
U16 = mybir.dt.uint16
U8 = mybir.dt.uint8
FP8X4 = mybir.dt.float8_e4m3fn_x4
RELU = mybir.ActivationFunctionType.Relu
MULT = mybir.AluOpType.mult

P = 128
PACK = 4
K_PASS = P * PACK
K_PASSES = K // K_PASS
H_PASSES = H // K_PASS
N_TILES = N // P
SHARE = 40
LAST_SHARE = 72
RAW_COLS = PACK * H


def tile_routed_moe_kernel(tc, xT, w1, w2, gate, offs, out):
    nc = tc.nc

    with ExitStack() as ctx:
        keep = ctx.enter_context(tc.tile_pool(name="keep", bufs=1))
        ring = ctx.enter_context(tc.tile_pool(name="ring", bufs=6))
        mid = ctx.enter_context(tc.tile_pool(name="mid", bufs=3))
        codes = ctx.enter_context(tc.tile_pool(name="codes", bufs=2))
        psum = ctx.enter_context(tc.psum_pool(name="psum", bufs=2))

        offsets = keep.tile([P, E * C // 16], U16, name="offsets")
        gate_sb = keep.tile([P, N_TILES, E * C], F32, name="gate_sb")
        windows = [keep.tile([P, T], F32, name=f"window{n}") for n in range(N_TILES)]
        x_words = [keep.tile([P, T], U32, name=f"x_words{s}", align_bytes=64) for s in range(K_PASSES)]
        x_bytes = [keep.tile([P, T], U8, name=f"x_bytes{s}", align_bytes=64) for s in range(K_PASSES)]
        g_words = [keep.tile([P, E * C], U32, name=f"g_words{s}", align_bytes=64) for s in range(K_PASSES)]
        g_bytes = [keep.tile([P, E * C], U8, name=f"g_bytes{s}", align_bytes=64) for s in range(K_PASSES)]

        def load(rows, width):
            raw = ring.tile([P, RAW_COLS], F32, name="raw")
            view = raw[:, : PACK * width].rearrange("p (j w) -> p j w", j=PACK)
            nc.sync.dma_start(view, rows.rearrange("(p j) w -> p j w", j=PACK))
            return view

        def interleave(copy, grouped, view):
            copy(
                grouped.rearrange("p (c i j) -> p c j i", i=PACK, j=PACK),
                view.rearrange("p j (c i) -> p c j i", i=PACK),
            )

        def interleave_permuted(copy, grouped, view, m0, m1):
            copy(
                grouped.rearrange("p (b t m j) -> p b m j t", t=PACK, m=P, j=PACK)[:, :, m0:m1],
                view.rearrange("p j (b m t) -> p b m j t", m=P, t=PACK)[:, :, m0:m1],
            )

        for s in range(K_PASSES):
            nc.gpsimd.memset(x_bytes[s][:], 0)
        for s in range(K_PASSES):
            view = load(xT[K_PASS * s : K_PASS * (s + 1), :], T)
            if s == 0:
                nc.sync.dma_start(offsets[:], offs)
            half = T // 2
            for i, copy in enumerate((nc.vector.tensor_copy, nc.scalar.copy)):
                cols = slice(half * i, half * (i + 1))
                grouped = mid.tile([P, PACK * half], BF16, name=f"x_grouped{i}", align_bytes=64)
                interleave(copy, grouped[:], view[:, :, cols])
                nc.vector.quantize_mx(
                    out=x_words[s][:, cols].bitcast(FP8X4), scales=x_bytes[s][:, cols], in_=grouped[:]
                )
        for s in range(K_PASSES):
            for g0 in range(0, E * C, 256):
                some = offsets[:, g0 // 16 : (g0 + 256) // 16]
                nc.vector.tensor_copy(g_words[s][:, g0 : g0 + 256], x_words[s][:].indirect(some))
                nc.vector.tensor_copy(g_bytes[s][:, g0 : g0 + 256], x_bytes[s][:].indirect(some))

        def first_layer(e):
            slots = slice(C * e, C * (e + 1))
            w_words, w_bytes, grouped_tiles = [], [], []

            def quantize(s, c0, c1):
                nc.vector.quantize_mx(
                    out=w_words[s][:, c0:c1].bitcast(FP8X4),
                    scales=w_bytes[s][:, c0:c1],
                    in_=grouped_tiles[s][:, PACK * c0 : PACK * c1],
                )

            for s in range(K_PASSES):
                rows = w1[e, K_PASS * s : K_PASS * (s + 1), :]
                w_words.append(codes.tile([P, H], U32, name=f"w1_words{s}", align_bytes=64))
                w_bytes.append(codes.tile([P, H], U8, name=f"w1_bytes{s}", align_bytes=64))
                grouped = mid.tile([P, PACK * H], BF16, name="w1_grouped", align_bytes=64)
                grouped_tiles.append(grouped)
                if e == E - 1 and s == K_PASSES - 1:
                    quantize(s - 1, 0, H)
                    for b in range(H_PASSES):
                        half = load(rows[:, K_PASS * b : K_PASS * (b + 1)], K_PASS)
                        part = grouped[:, PACK * K_PASS * b : PACK * K_PASS * (b + 1)]
                        interleave_permuted(nc.vector.tensor_copy, part, half, 0, LAST_SHARE)
                        interleave_permuted(nc.scalar.copy, part, half, LAST_SHARE, P)
                        quantize(s, K_PASS * b, K_PASS * (b + 1))
                else:
                    view = load(rows, H)
                    interleave_permuted(nc.vector.tensor_copy, grouped[:], view, 0, SHARE)
                    interleave_permuted(nc.scalar.copy, grouped[:], view, SHARE, P)
                    if s > 0:
                        quantize(s - 1, 0, H)
                    if s == K_PASSES - 1:
                        quantize(s, 0, H)
            hidden = []
            for b in range(H_PASSES):
                acc = psum.tile([P, PACK, C], F32, name=f"h_acc{b}")
                for t in range(PACK):
                    cols = slice(K_PASS * b + P * t, K_PASS * b + P * (t + 1))
                    for s in range(K_PASSES):
                        nc.tensor.matmul_mx(
                            out=acc[:, t, :],
                            lhsT=w_words[s][:, cols].bitcast(FP8X4),
                            lhsT_scale=w_bytes[s][:, cols],
                            rhs=g_words[s][:, slots].bitcast(FP8X4),
                            rhs_scale=g_bytes[s][:, slots],
                            start=(s == 0),
                            stop=(s == K_PASSES - 1),
                        )
                h_grouped = codes.tile([P, C, PACK], BF16, name=f"h_grouped{b}", align_bytes=64)
                nc.scalar.activation(h_grouped[:], acc[:].rearrange("p t n -> p n t"), RELU)
                words = codes.tile([P, C], U32, name=f"h_words{b}", align_bytes=64)
                scales = codes.tile([P, C], U8, name=f"h_bytes{b}", align_bytes=64)
                nc.vector.quantize_mx(
                    out=words[:].bitcast(FP8X4), scales=scales[:], in_=h_grouped[:].rearrange("p n t -> p (n t)")
                )
                hidden.append((words, scales))
            return hidden

        def second_matmul(acc, w_words, w_bytes, hidden):
            for b in range(H_PASSES):
                nc.tensor.matmul_mx(
                    out=acc,
                    lhsT=w_words[b].bitcast(FP8X4),
                    lhsT_scale=w_bytes[b],
                    rhs=hidden[b][0][:].bitcast(FP8X4),
                    rhs_scale=hidden[b][1][:],
                    start=(b == 0),
                    stop=(b == H_PASSES - 1),
                )

        def back(e, n, weighted):
            nc.vector.tensor_copy(windows[n][:].indirect(offsets[:, C * e // 16 : C * (e + 1) // 16]), weighted)

        def second_layer(e, hidden):
            slots = slice(C * e, C * (e + 1))
            raw = ring.tile([P, RAW_COLS], F32, name="raw")
            view = raw[:, : H_PASSES * PACK * N].rearrange("p (s j n) -> p s j n", s=H_PASSES, j=PACK)
            nc.sync.dma_start(view, w2[e].rearrange("(s p j) n -> p s j n", s=H_PASSES, j=PACK))
            width = PACK * N
            grouped = codes.tile([P, H_PASSES * width], BF16, name="w2_grouped", align_bytes=64)
            words = codes.tile([P, H_PASSES * N], U32, name="w2_words", align_bytes=64)
            scales = codes.tile([P, H_PASSES * N], U8, name="w2_bytes", align_bytes=64)
            for s in range(H_PASSES):
                interleave(nc.scalar.copy, grouped[:, width * s : width * (s + 1)], view[:, s])
            for c0, c1 in ((0, 512), (512, 768)):
                nc.vector.quantize_mx(
                    out=words[:, c0:c1].bitcast(FP8X4), scales=scales[:, c0:c1], in_=grouped[:, PACK * c0 : PACK * c1]
                )
            acc = psum.tile([P, N_TILES, C], F32, name="y_acc")
            for n in range(N_TILES):
                cols = [slice(N * b + P * n, N * b + P * (n + 1)) for b in range(H_PASSES)]
                second_matmul(acc[:, n, :], [words[:, c] for c in cols], [scales[:, c] for c in cols], hidden)
            weighted = codes.tile([P, N_TILES, C], F32, name="weighted")
            nc.vector.tensor_tensor(weighted[:], acc[:], gate_sb[:, :, slots], MULT)
            for n in range(N_TILES):
                back(e, n, weighted[:, n, :])

        def last_second_layer(e, hidden):
            slots = slice(C * e, C * (e + 1))
            acc = psum.tile([P, N_TILES, C], F32, name="y_acc")
            for n0, n1 in ((0, 2), (2, 3)):
                width = P * (n1 - n0)
                w_words, w_bytes = [], []
                for s, copy in enumerate((nc.scalar.copy, nc.vector.tensor_copy)):
                    view = load(w2[e, K_PASS * s : K_PASS * (s + 1), P * n0 : P * n1], width)
                    grouped = codes.tile([P, PACK * width], BF16, name=f"w2_last_grouped{s}", align_bytes=64)
                    interleave(copy, grouped[:], view)
                    words = codes.tile([P, width], U32, name=f"w2_last_words{s}", align_bytes=64)
                    scales = codes.tile([P, width], U8, name=f"w2_last_bytes{s}", align_bytes=64)
                    nc.vector.quantize_mx(out=words[:].bitcast(FP8X4), scales=scales[:], in_=grouped[:])
                    w_words.append(words)
                    w_bytes.append(scales)
                for n in range(n0, n1):
                    cols = slice(P * (n - n0), P * (n - n0 + 1))
                    second_matmul(acc[:, n, :], [w[:, cols] for w in w_words], [w[:, cols] for w in w_bytes], hidden)
                weighted = codes.tile([P, n1 - n0, C], F32, name="weighted_last")
                nc.vector.tensor_tensor(weighted[:], acc[:, n0:n1, :], gate_sb[:, n0:n1, slots], MULT)
                for n in range(n0, n1):
                    back(e, n, weighted[:, n - n0, :])
                    nc.sync.dma_start(out[P * n : P * (n + 1), :], windows[n][:])

        hidden = first_layer(0)
        nc.sync.dma_start(gate_sb[:], gate.rearrange("(n p) j -> p n j", p=P))
        for e in range(E - 1):
            second_layer(e, hidden)
            hidden = first_layer(e + 1)
        last_second_layer(E - 1, hidden)
